import numpy as np
import ml_dtypes


def mxq(x, axis, fmt="e4m3"):
    dtype, down = {"e4m3": (ml_dtypes.float8_e4m3fn, 7), "e5m2": (ml_dtypes.float8_e5m2, 14)}[fmt]
    v = np.moveaxis(np.asarray(x, np.float32).astype(ml_dtypes.bfloat16).astype(np.float64), axis, -1)
    blocks = v.reshape(v.shape[:-1] + (-1, 32))
    amax = np.abs(blocks).max(-1, keepdims=True)
    byte = np.maximum(np.where(amax > 0, np.frexp(amax)[1] - 1 + 127, 0) - down, 1)
    scale = np.exp2(byte - 127.0)
    codes = (blocks / scale).astype(np.float32).astype(dtype).astype(np.float64)
    return np.moveaxis((codes * scale).reshape(v.shape), -1, axis)


WIDE = False


def mx_kscale(k):
    if not WIDE:
        return np.ones(k)
    levels = np.array([10, -10, 5, -5, 0])
    if k % 512:
        return np.exp2(np.random.permutation(np.resize(levels, k // 32))).repeat(32)
    a = np.empty((k // 512, 16))
    for p in range(k // 512):
        a[p, :8] = np.random.permutation(np.resize(levels, 8))
        for g in range(8):
            far = levels[np.abs(levels - a[p, g]) >= 10]
            a[p, g + 8] = far[np.random.randint(len(far))]
    return np.exp2(a.ravel()).repeat(32)


BF16 = ml_dtypes.bfloat16


def bf(x):
    return np.asarray(x, np.float32).astype(BF16)


def f64(x):
    return np.asarray(x).astype(np.float64)


N, D, F = 1024, 512, 2048


def silu_with_tangent(pre, dpre):
    s = 1.0 / (1.0 + np.exp(-pre))
    h = pre * s
    dh = s * (1.0 + pre * (1.0 - s)) * dpre
    return h, dh


def draw0():
    s, t = mx_kscale(D), mx_kscale(F)
    return {
        "z": bf(np.random.standard_normal((N, D)) * 0.7),
        "v": bf(np.random.standard_normal((N, D)) * 0.8),
        "tau": bf(np.random.uniform(0.2, 1.0, N)),
        "gin": bf((1.0 + 0.1 * np.random.standard_normal(D)) * s),
        "w1": bf(np.random.standard_normal((D, F)) / np.sqrt(D) / s[:, None]),
        "gf": bf((1.0 + 0.1 * np.random.standard_normal(F)) * t),
        "w2": bf(np.random.standard_normal((F, D)) * 1.5 / np.sqrt(F) / t[:, None]),
    }


def core(z, v, tau, gin, w1, gf, w2):
    z, v, gin, gf = f64(z), f64(v), f64(gin), f64(gf)
    tau_col = f64(tau)[:, None]

    zin = (1.0 + tau_col) * z * gin[None, :]
    dzin = ((1.0 + tau_col) * v + z) * gin[None, :]

    w1q = mxq(f64(w1), 0, "e4m3")
    pre = mxq(zin, 1, "e4m3") @ w1q
    dpre = mxq(dzin, 1, "e4m3") @ w1q

    h, dh = silu_with_tangent(pre, dpre)

    m = (h + tau_col * dh) * gf[None, :]

    err = (mxq(m, 1, "e4m3") @ mxq(f64(w2), 0, "e4m3")) - v

    q = np.mean(err * err, axis=-1)
    wgt = (q + 0.1) ** -0.75
    return wgt[:, None] * err


def e4m3fn_bytes(y):
    return np.clip(np.asarray(y, np.float64), -448.0, 448.0).astype(np.float32).astype(ml_dtypes.float8_e4m3fn).view(np.uint8)


def e4m3fn_values(b):
    return np.asarray(b, np.uint8).view(ml_dtypes.float8_e4m3fn).astype(np.float64)


def setup_inputs():
    d = draw0()
    x0 = np.asarray(d['w2']).astype(np.float64)
    s = (np.max(np.abs(x0), axis=(1,), keepdims=True) / 448.0).astype(np.float32)
    out = {}
    for k, v in d.items():
        if k == 'w2':
            out['w2_bytes'] = e4m3fn_bytes(x0 / s.astype(np.float64))
            out['w2_scale'] = s
        else:
            out[k] = v
    return out


def reference(z, v, tau, gin, w1, gf, w2_bytes, w2_scale):
    return core(z, v, tau, gin, w1, gf, e4m3fn_values(w2_bytes) * w2_scale.astype(np.float64))

@@ -1,0 +1,385 @@
+from contextlib import ExitStack
+
+import concourse.mybir as mybir
+from concourse.masks import make_identity
+
+N, D, F = 1024, 512, 2048
+FLOPS = 3 * 2 * N * D * F
+
+F32 = mybir.dt.float32
+BF16 = mybir.dt.bfloat16
+U32 = mybir.dt.uint32
+U8 = mybir.dt.uint8
+FP8 = mybir.dt.float8_e4m3fn
+FP8X4 = mybir.dt.float8_e4m3fn_x4
+ALU = mybir.AluOpType
+ACT = mybir.ActivationFunctionType
+
+P = 128
+PACK = 4
+K_PASS = P * PACK
+TILES = N // P
+GROUPS = F // K_PASS
+STEPS = TILES * GROUPS
+V1_POOL = False
+OUT_POOL = False
+W1_IL = "vvvv"
+W2_IL = "ssss"
+HEAD_PIECES = 5
+PIECE_RATE = 2
+LAG = 2
+YLAG = 2
+RT_ENGINE = "vs"*7+"s"*18
+
+
+def interleaved(dst, src):
+    return (dst.rearrange("p (c i) t -> p c t i", i=4), src.rearrange("p t (c i) -> p c t i", i=4))
+
+
+def tile_meanflowtangentresidual_kernel(tc, z, v, tau, gin, w1, gf, w2_bytes, w2_scale, out):
+    nc = tc.nc
+    z_rows = z.rearrange("(p i) d -> p i d", i=TILES)
+    v_rows = v.rearrange("(p i) d -> p i d", i=TILES)
+    out_rows = out.rearrange("(p i) d -> p i d", i=TILES)
+
+    with ExitStack() as ctx:
+        keep = ctx.enter_context(tc.tile_pool(name="keep", bufs=1))
+        work = ctx.enter_context(tc.tile_pool(name="work", bufs=3))
+        psum = ctx.enter_context(tc.psum_pool(name="psum", bufs=1))
+        ctx.enter_context(tc.manual_schedule())
+
+        tau_bf = keep.tile([P, TILES], BF16)
+        gin_bf = keep.tile([P, PACK], BF16)
+        gf_bf = keep.tile([P, GROUPS, PACK], BF16)
+        w2_sc = keep.tile([P, GROUPS, PACK], F32)
+        z_sb = [keep.tile([P, D], BF16, name="z%d" % i) for i in range(TILES)]
+        v_sb = [keep.tile([P, D], BF16, name="v%d" % i) for i in range(TILES)]
+        w1_raw = [keep.tile([P, PACK, K_PASS], BF16, name="w1raw%d" % g) for g in range(GROUPS)]
+        w2_raw = [keep.tile([P, PACK * D], U8, name="w2raw%d" % g) for g in range(GROUPS)]
+        w1_rows = w1.rearrange("(p j) f -> p j f", j=PACK)
+        w2_rows = w2_bytes.rearrange("(g p t) n -> g p (t n)", p=P, t=PACK)
+
+        def load_tokens(i):
+            nc.sync.dma_start(out=z_sb[i][:], in_=z_rows[:, i, :])
+            nc.sync.dma_start(out=v_sb[i][:], in_=v_rows[:, i, :])
+
+        def load_w1(g):
+            nc.sync.dma_start(out=w1_raw[g][:], in_=w1_rows[:, :, g * K_PASS:(g + 1) * K_PASS])
+
+        def load_w2(g):
+            nc.sync.dma_start(out=w2_raw[g][:], in_=w2_rows[g])
+
+        nc.sync.dma_start(out=tau_bf[:], in_=tau.rearrange("(p i) -> p i", i=TILES))
+        load_tokens(0)
+        load_w1(0)
+        nc.sync.dma_start(out=gin_bf[:], in_=gin.rearrange("(p t) -> p t", t=PACK))
+        nc.sync.dma_start(out=w2_sc[:], in_=w2_scale.rearrange("(g p t) o -> p g (t o)", p=P, t=PACK))
+        load_w2(0)
+        load_w1(1)
+        nc.sync.dma_start(out=gf_bf[:], in_=gf.rearrange("(g p t) -> p g t", p=P, t=PACK))
+        load_tokens(1)
+        for g in range(1, GROUPS):
+            if g + 1 < GROUPS:
+                load_w1(g + 1)
+            load_w2(g)
+        for i in range(2, TILES):
+            load_tokens(i)
+
+        warm = keep.tile([P, 1], F32)
+        warm_out = keep.tile([P, 1], F32)
+        nc.vector.memset(warm[:], 0.0)
+        nc.scalar.activation(out=warm_out[:], in_=warm[:], func=ACT.Silu)
+        ident_bf = keep.tile([P, P], BF16)
+        ident_f = keep.tile([P, P], F32)
+        make_identity(nc, ident_bf[:])
+        make_identity(nc, ident_f[:])
+        power = keep.tile([P, 1], F32)
+        nc.gpsimd.memset(power[:], -0.75)
+        tau_f = keep.tile([P, TILES], F32)
+        tau_1 = keep.tile([P, TILES], F32)
+        tau_h = keep.tile([P, TILES], F32)
+        tau_nh = keep.tile([P, TILES], F32)
+        nc.vector.tensor_scalar(out=tau_1[:], in0=tau_bf[:], scalar1=1.0, scalar2=None, op0=ALU.add)
+        nc.vector.tensor_copy(out=tau_f[:], in_=tau_bf[:])
+        nc.vector.tensor_scalar(out=tau_h[:], in0=tau_bf[:], scalar1=0.5, scalar2=None, op0=ALU.mult)
+        nc.vector.tensor_scalar(out=tau_nh[:], in0=tau_bf[:], scalar1=-0.5, scalar2=None, op0=ALU.mult)
+        diag = keep.tile([P, TILES, P], BF16)
+        for i in range(TILES):
+            nc.gpsimd.tensor_scalar(out=diag[:, i, :], in0=ident_bf[:], scalar1=tau_f[:, i:i + 1], scalar2=0.0,
+                                    op0=ALU.mult, op1=ALU.add)
+
+        w1_codes = keep.tile([P, GROUPS, K_PASS], U32, align_bytes=64)
+        w1_scales = keep.tile([P, GROUPS, K_PASS], U8, align_bytes=64)
+        w2_codes = keep.tile([P, GROUPS, D], U32, align_bytes=64)
+        w2_scales = keep.tile([P, GROUPS, D], U8, align_bytes=64)
+        x_codes = keep.tile([P, TILES, 2 * P], U32, align_bytes=64)
+        x_scales = keep.tile([P, TILES, 2 * P], U8, align_bytes=64)
+        m_codes = keep.tile([P, STEPS, P], U32, align_bytes=64)
+        m_scales = keep.tile([P, STEPS, P], U8, align_bytes=64)
+
+        live = {}
+
+        def quantize(codes, scales, values):
+            nc.vector.quantize_mx(out=codes.bitcast(FP8X4), scales=scales, in_=values)
+
+        def copy_on(engine, dst, src):
+            if engine == "v":
+                nc.vector.tensor_copy(out=dst, in_=src)
+            elif engine == "s":
+                nc.scalar.copy(out=dst, in_=src)
+            else:
+                nc.gpsimd.tensor_scalar(out=dst, in0=src, scalar1=1.0, scalar2=0.0, op0=ALU.mult, op1=ALU.add)
+
+        def affine_on(engine, dst, src, scale, bias):
+            if engine == "s" and bias is None:
+                nc.scalar.activation(out=dst, in_=src, func=ACT.Copy, scale=scale)
+            elif engine == "s":
+                nc.scalar.activation(out=dst, in_=src, func=ACT.Identity, scale=scale, bias=bias)
+            elif engine == "v":
+                nc.vector.tensor_scalar(out=dst, in0=src, scalar1=scale, scalar2=0.0 if bias is None else bias,
+                                        op0=ALU.mult, op1=ALU.add)
+            else:
+                nc.gpsimd.tensor_scalar(out=dst, in0=src, scalar1=scale, scalar2=0.0 if bias is None else bias,
+                                        op0=ALU.mult, op1=ALU.add)
+
+        def w1_interleave(g):
+            w1_il = work.tile([P, K_PASS, PACK], BF16, bufs=2, align_bytes=64)
+            dst, src = interleaved(w1_il[:], w1_raw[g][:])
+            copy_on(W1_IL[g], dst, src)
+            live["w1_il", g] = w1_il
+
+        def w1_quantize(g):
+            quantize(w1_codes[:, g, :], w1_scales[:, g, :], live["w1_il", g][:].rearrange("p n t -> p (n t)"))
+
+        def w2_piece(n):
+            g, t = divmod(n, 2 * PACK)
+            if t == 0:
+                live["w2_wide", g] = work.tile([P, PACK, D], BF16, bufs=2, name="w2_wide")
+            if t == PACK:
+                live["w2_il", g] = work.tile([P, D, PACK], BF16, bufs=2, align_bytes=64, name="w2_il")
+            if t < PACK:
+                nc.scalar.activation(out=live["w2_wide", g][:, t, :], in_=w2_raw[g][:, t * D:(t + 1) * D].bitcast(FP8),
+                                     func=ACT.Copy, scale=w2_sc[:, g, t:t + 1])
+            else:
+                cols = slice((t - PACK) * P, (t - PACK + 1) * P)
+                dst, src = interleaved(live["w2_il", g][:, cols, :], live["w2_wide", g][:, :, cols])
+                copy_on(W2_IL[g], dst, src)
+
+        def w2_quantize(g):
+            quantize(w2_codes[:, g, :], w2_scales[:, g, :], live["w2_il", g][:].rearrange("p n t -> p (n t)"))
+
+        def scale_v(i):
+            v1 = work.tile([P, PACK, P], F32, bufs=2)
+            affine_on("g" if V1_POOL and i > 0 else "s", v1[:], v_sb[i][:].rearrange("p (m t) -> p t m", t=PACK),
+                      tau_1[:, i:i + 1], None)
+            live["v1", i] = v1
+
+        def turn_z(i):
+            x_bank = psum.tile([P, PACK, P], F32, tag="x_bank")
+            for t in range(PACK):
+                z_t = z_sb[i][:, t::PACK]
+                nc.tensor.matmul(x_bank[:, t, :], lhsT=z_t, rhs=ident_bf[:], start=True, stop=False)
+                nc.tensor.matmul(x_bank[:, t, :], lhsT=z_t, rhs=diag[:, i, :], start=False, stop=True)
+            live["x_bank", i, 0] = x_bank
+
+        def turn_dz(i):
+            if i == 0:
+                x_bank = psum.tile([P, PACK, P], F32, tag="acc", bufs=2)
+            else:
+                x_bank = psum.tile([P, PACK, P], F32, tag="x_bank")
+            for t in range(PACK):
+                nc.tensor.matmul(x_bank[:, t, :], lhsT=z_sb[i][:, t::PACK], rhs=ident_bf[:], start=True, stop=False)
+                nc.tensor.matmul(x_bank[:, t, :], lhsT=live["v1", i][:, t, :], rhs=ident_f[:], start=False, stop=True,
+                                 is_transpose=True)
+            live["x_bank", i, 1] = x_bank
+
+        def gain_in(i, which):
+            if which == 0:
+                live["x_il", i] = work.tile([P, 2, P, PACK], BF16, bufs=2, align_bytes=64, name="x_il")
+            nc.vector.tensor_tensor(out=live["x_il", i][:, which, :, :],
+                                    in0=live["x_bank", i, which][:].rearrange("p t n -> p n t"),
+                                    in1=gin_bf[:].unsqueeze(1).to_broadcast([P, P, PACK]), op=ALU.mult)
+
+        def x_quantize(i):
+            quantize(x_codes[:, i, :], x_scales[:, i, :], live["x_il", i][:].rearrange("p o n t -> p (o n t)"))
+
+        def x_quantize_half(i, which):
+            cols = slice(which * P, (which + 1) * P)
+            quantize(x_codes[:, i, cols], x_scales[:, i, cols], live["x_il", i][:, which].rearrange("p n t -> p (n t)"))
+
+        def project(s, which, tag, bufs):
+            i, g = divmod(s, GROUPS)
+            bank = psum.tile([P, K_PASS], F32, tag=tag, bufs=bufs, name=tag)
+            cols = slice(which * P, (which + 1) * P)
+            nc.tensor.matmul_mx(out=bank[:], lhsT=x_codes[:, i, cols].bitcast(FP8X4), lhsT_scale=x_scales[:, i, cols],
+                                rhs=w1_codes[:, g, :].bitcast(FP8X4), rhs_scale=w1_scales[:, g, :],
+                                start=True, stop=True)
+            live[tag, s] = bank
+
+        def activations(s):
+            i = s // GROUPS
+            pre = live["pre", s][:].rearrange("p (m t) -> p t m", t=PACK)
+            th = work.tile([P, PACK, P], F32, bufs=LAG + 1)
+            h = work.tile([P, PACK, P], F32, bufs=LAG + 3)
+            rt = work.tile([P, PACK, P], F32, bufs=LAG + 2)
+            nc.scalar.activation(out=th[:], in_=pre, func=ACT.Tanh, scale=0.5)
+            nc.scalar.activation(out=h[:], in_=pre, func=ACT.Silu)
+            if RT_ENGINE[s] != "v":
+                affine_on(RT_ENGINE[s], rt[:], th[:], tau_nh[:, i:i + 1], tau_h[:, i:i + 1])
+            live["th", s] = th
+            live["h", s] = h
+            live["rt", s] = rt
+
+        def rt_on_vector(s):
+            i = s // GROUPS
+            if RT_ENGINE[s] == "v":
+                affine_on("v", live["rt", s][:], live["th", s][:], tau_nh[:, i:i + 1], tau_h[:, i:i + 1])
+
+        def slope(s):
+            x = work.tile([P, PACK, P], F32, bufs=2)
+            nc.vector.scalar_tensor_tensor(out=x[:], in0=live["h", s][:], scalar=-1.0, in1=live["rt", s][:],
+                                           op0=ALU.add, op1=ALU.mult)
+            live["x", s] = x
+
+        def tangent(s):
+            i = s // GROUPS
+            a = work.tile([P, PACK, P], F32, bufs=3)
+            nc.vector.scalar_tensor_tensor(out=a[:], in0=live["x", s][:], scalar=tau_f[:, i:i + 1],
+                                           in1=live["dpre", s][:].rearrange("p (m t) -> p t m", t=PACK),
+                                           op0=ALU.add, op1=ALU.mult)
+            live["a", s] = a
+
+        def turn_hidden(s):
+            y_bank = psum.tile([P, PACK, P], F32, bufs=2)
+            for t in range(PACK):
+                nc.tensor.matmul(y_bank[:, t, :], lhsT=live["h", s][:, t, :], rhs=ident_f[:], start=True, stop=False,
+                                 is_transpose=True)
+                nc.tensor.matmul(y_bank[:, t, :], lhsT=live["a", s][:, t, :], rhs=ident_f[:], start=False, stop=True,
+                                 is_transpose=True)
+            live["y_bank", s] = y_bank
+
+        def gain_hidden(s):
+            g = s % GROUPS
+            m_il = work.tile([P, P, PACK], BF16, bufs=2, align_bytes=64)
+            nc.vector.tensor_tensor(out=m_il[:], in0=live["y_bank", s][:].rearrange("p t n -> p n t"),
+                                    in1=gf_bf[:, g, :].unsqueeze(1).to_broadcast([P, P, PACK]), op=ALU.mult)
+            live["m_il", s] = m_il
+
+        def m_quantize(s):
+            quantize(m_codes[:, s, :], m_scales[:, s, :], live["m_il", s][:].rearrange("p n t -> p (n t)"))
+
+        def second_pass(s):
+            i, g = divmod(s, GROUPS)
+            if g == 0:
+                live["acc", i] = psum.tile([P, D], F32, bufs=2, name="acc", tag="acc")
+            nc.tensor.matmul_mx(out=live["acc", i][:], lhsT=m_codes[:, s, :].bitcast(FP8X4), lhsT_scale=m_scales[:, s, :],
+                                rhs=w2_codes[:, g, :].bitcast(FP8X4), rhs_scale=w2_scales[:, g, :],
+                                start=(g == 0), stop=(g == GROUPS - 1))
+
+        def residual(i):
+            err = work.tile([P, D], F32, bufs=3)
+            nc.vector.tensor_tensor(out=err[:], in0=live["acc", i][:], in1=v_sb[i][:], op=ALU.subtract)
+            live["err", i] = err
+
+        def weight(i):
+            squares = work.tile([P, D], BF16, bufs=2)
+            total = work.tile([P, 1], F32, bufs=2)
+            base = work.tile([P, 1], F32, bufs=2)
+            wgt = work.tile([P, 1], F32, bufs=2)
+            nc.scalar.activation(out=squares[:], in_=live["err", i][:], func=ACT.Square, accum_out=total[:])
+            nc.gpsimd.tensor_scalar(out=base[:], in0=total[:], scalar1=1.0 / D, scalar2=0.1, op0=ALU.mult, op1=ALU.add)
+            nc.gpsimd.tensor_tensor(out=wgt[:], in0=base[:], in1=power[:], op=ALU.pow)
+            live["wgt", i] = wgt
+
+        def finish(i):
+            result = work.tile([P, D], F32, bufs=2)
+            affine_on("v" if i == TILES - 1 else "g" if OUT_POOL else "s", result[:], live["err", i][:], live["wgt", i][:], None)
+            nc.sync.dma_start(out=out_rows[:, i, :], in_=result[:])
+
+        def at(k, first, period, count):
+            n, rest = divmod(k - first, period)
+            return [n] if rest == 0 and 0 <= n < count else []
+
+        scale_v(0)
+        turn_z(0)
+        turn_dz(0)
+        gain_in(0, 0)
+        w1_interleave(0)
+        x_quantize_half(0, 0)
+        w1_quantize(0)
+        gain_in(0, 1)
+        w1_interleave(1)
+        x_quantize_half(0, 1)
+        w1_quantize(1)
+
+        for n in range(HEAD_PIECES):
+            w2_piece(n)
+        pieces = HEAD_PIECES
+        w2_done = 0
+        w2_ready = {}
+        next_pass = 0
+        closed = {}
+        FIN = LAG + YLAG
+        for k in range(-1, STEPS + FIN + 8):
+            for s in at(k, 0, 1, STEPS):
+                activations(s)
+            for i in at(k, 0, GROUPS, TILES - 1):
+                scale_v(i + 1)
+            for g in range(2, GROUPS):
+                if W1_IL[g] != "v" and k == g - 3:
+                    w1_interleave(g)
+            before = pieces
+            while pieces < 2 * PACK * GROUPS and pieces < HEAD_PIECES + PIECE_RATE * (k + 1):
+                w2_piece(pieces)
+                pieces = pieces + 1
+            if k - 3 in closed and closed[k - 3] < TILES - 1:
+                finish(closed[k - 3])
+            if k - 2 in closed:
+                weight(closed[k - 2])
+            for s in at(k, LAG, 1, STEPS):
+                slope(s)
+            for s in at(k, FIN, 1, STEPS):
+                gain_hidden(s)
+            for g in at(k, 0, 1, 2):
+                w1_quantize(g + 2)
+            for s in at(k, LAG, 1, STEPS):
+                tangent(s)
+            for i in at(k, 1, GROUPS, TILES - 1):
+                gain_in(i + 1, 0)
+            for i in at(k, 2, GROUPS, TILES - 1):
+                gain_in(i + 1, 1)
+            for s in at(k, FIN, 1, STEPS):
+                m_quantize(s)
+            for g in range(2, GROUPS):
+                if W1_IL[g] == "v" and k == g - 3:
+                    w1_interleave(g)
+            if before >= 2 * PACK * (w2_done + 1):
+                w2_quantize(w2_done)
+                w2_ready[w2_done] = k
+                w2_done = w2_done + 1
+            for i in at(k, 2, GROUPS, TILES - 1):
+                x_quantize(i + 1)
+            if k - 1 in closed:
+                residual(closed[k - 1])
+            if k - 3 in closed and closed[k - 3] == TILES - 1:
+                finish(closed[k - 3])
+            for s in at(k, LAG - 1, 1, STEPS):
+                rt_on_vector(s)
+            for s in at(k, -1, 1, STEPS):
+                project(s, 0, "pre", 2)
+            for twice in range(2):
+                s = next_pass
+                if s < STEPS and k > s + FIN and k > w2_ready.get(s % GROUPS, k) and k not in closed:
+                    second_pass(s)
+                    next_pass = s + 1
+                    if s % GROUPS == GROUPS - 1:
+                        closed[k] = s // GROUPS
+            for s in at(k, LAG - 1, 1, STEPS):
+                project(s, 1, "dpre", 1)
+            for i in at(k, 0, GROUPS, TILES - 1):
+                turn_z(i + 1)
+            for i in at(k, 1, GROUPS, TILES - 1):
+                turn_dz(i + 1)
+            for s in at(k, LAG, 1, STEPS):
+                turn_hidden(s)
+        assert next_pass == STEPS and len(closed) == TILES

@@ -22,14 +22,22 @@ TILES = N // P
 GROUPS = F // K_PASS
 STEPS = TILES * GROUPS
 V1_POOL = False
+V1_TILES = 1
+OUT_ENGINE = "sssssssv"
 OUT_POOL = False
 W1_IL = "vvvv"
 W2_IL = "ssss"
-HEAD_PIECES = 5
-PIECE_RATE = 2
+HEAD_PIECES = 12
+PIECE_RATE = 1
 LAG = 2
 YLAG = 2
-RT_ENGINE = "vs"*7+"s"*18
+PASSES = 2
+D_BUFS = 2
+RT_BUFS = 1
+GAIN_ENGINE = "v" * 32
+LOADS = "tau x0 a0 sc b0 gin a1 gf x1 a2 b1 a3 b2 b3 x2 x3 x4 x5 x6 x7"
+PRE_PIECES = 0
+RT_ENGINE = "s" * 32
 
 
 def interleaved(dst, src):
@@ -69,21 +77,21 @@ def tile_meanflowtangentresidual_kernel(tc, z, v, tau, gin, w1, gf, w2_bytes, w2
         def load_w2(g):
             nc.sync.dma_start(out=w2_raw[g][:], in_=w2_rows[g])
 
-        nc.sync.dma_start(out=tau_bf[:], in_=tau.rearrange("(p i) -> p i", i=TILES))
-        load_tokens(0)
-        load_w1(0)
-        nc.sync.dma_start(out=gin_bf[:], in_=gin.rearrange("(p t) -> p t", t=PACK))
-        nc.sync.dma_start(out=w2_sc[:], in_=w2_scale.rearrange("(g p t) o -> p g (t o)", p=P, t=PACK))
-        load_w2(0)
-        load_w1(1)
-        nc.sync.dma_start(out=gf_bf[:], in_=gf.rearrange("(g p t) -> p g t", p=P, t=PACK))
-        load_tokens(1)
-        for g in range(1, GROUPS):
-            if g + 1 < GROUPS:
-                load_w1(g + 1)
-            load_w2(g)
-        for i in range(2, TILES):
-            load_tokens(i)
+        for item in LOADS.split():
+            if item == "tau":
+                nc.sync.dma_start(out=tau_bf[:], in_=tau.rearrange("(p i) -> p i", i=TILES))
+            elif item == "gin":
+                nc.sync.dma_start(out=gin_bf[:], in_=gin.rearrange("(p t) -> p t", t=PACK))
+            elif item == "sc":
+                nc.sync.dma_start(out=w2_sc[:], in_=w2_scale.rearrange("(g p t) o -> p g (t o)", p=P, t=PACK))
+            elif item == "gf":
+                nc.sync.dma_start(out=gf_bf[:], in_=gf.rearrange("(g p t) -> p g t", p=P, t=PACK))
+            elif item.startswith("a"):
+                load_w1(int(item.replace("a", "")))
+            elif item.startswith("b"):
+                load_w2(int(item.replace("b", "")))
+            else:
+                load_tokens(int(item.replace("x", "")))
 
         warm = keep.tile([P, 1], F32)
         warm_out = keep.tile([P, 1], F32)
@@ -99,14 +107,13 @@ def tile_meanflowtangentresidual_kernel(tc, z, v, tau, gin, w1, gf, w2_bytes, w2
         tau_1 = keep.tile([P, TILES], F32)
         tau_h = keep.tile([P, TILES], F32)
         tau_nh = keep.tile([P, TILES], F32)
+        diag = keep.tile([P, TILES, P], BF16)
         nc.vector.tensor_scalar(out=tau_1[:], in0=tau_bf[:], scalar1=1.0, scalar2=None, op0=ALU.add)
         nc.vector.tensor_copy(out=tau_f[:], in_=tau_bf[:])
         nc.vector.tensor_scalar(out=tau_h[:], in0=tau_bf[:], scalar1=0.5, scalar2=None, op0=ALU.mult)
         nc.vector.tensor_scalar(out=tau_nh[:], in0=tau_bf[:], scalar1=-0.5, scalar2=None, op0=ALU.mult)
-        diag = keep.tile([P, TILES, P], BF16)
-        for i in range(TILES):
-            nc.gpsimd.tensor_scalar(out=diag[:, i, :], in0=ident_bf[:], scalar1=tau_f[:, i:i + 1], scalar2=0.0,
-                                    op0=ALU.mult, op1=ALU.add)
+        nc.vector.tensor_tensor(out=diag[:], in0=ident_bf[:].unsqueeze(1).to_broadcast([P, TILES, P]),
+                                in1=tau_bf[:].unsqueeze(2).to_broadcast([P, TILES, P]), op=ALU.mult)
 
         w1_codes = keep.tile([P, GROUPS, K_PASS], U32, align_bytes=64)
         w1_scales = keep.tile([P, GROUPS, K_PASS], U8, align_bytes=64)
@@ -182,15 +189,22 @@ def tile_meanflowtangentresidual_kernel(tc, z, v, tau, gin, w1, gf, w2_bytes, w2
                 nc.tensor.matmul(x_bank[:, t, :], lhsT=z_t, rhs=diag[:, i, :], start=False, stop=True)
             live["x_bank", i, 0] = x_bank
 
-        def turn_dz(i):
-            if i == 0:
-                x_bank = psum.tile([P, PACK, P], F32, tag="acc", bufs=2)
+        def turn_dz(i, half):
+            if half == 1:
+                x_bank = live["x_bank", i, 1]
+            elif i == 0:
+                x_bank = psum.tile([P, PACK, P], F32, tag="acc", bufs=3 - D_BUFS)
             else:
                 x_bank = psum.tile([P, PACK, P], F32, tag="x_bank")
-            for t in range(PACK):
+            for t in range(2 * half, 2 * half + 2):
                 nc.tensor.matmul(x_bank[:, t, :], lhsT=z_sb[i][:, t::PACK], rhs=ident_bf[:], start=True, stop=False)
-                nc.tensor.matmul(x_bank[:, t, :], lhsT=live["v1", i][:, t, :], rhs=ident_f[:], start=False, stop=True,
-                                 is_transpose=True)
+                if i < V1_TILES:
+                    nc.tensor.matmul(x_bank[:, t, :], lhsT=live["v1", i][:, t, :], rhs=ident_f[:], start=False, stop=True,
+                                     is_transpose=True)
+                else:
+                    v_t = v_sb[i][:, t::PACK]
+                    nc.tensor.matmul(x_bank[:, t, :], lhsT=v_t, rhs=ident_bf[:], start=False, stop=False)
+                    nc.tensor.matmul(x_bank[:, t, :], lhsT=v_t, rhs=diag[:, i, :], start=False, stop=True)
             live["x_bank", i, 1] = x_bank
 
         def gain_in(i, which):
@@ -221,19 +235,21 @@ def tile_meanflowtangentresidual_kernel(tc, z, v, tau, gin, w1, gf, w2_bytes, w2
             pre = live["pre", s][:].rearrange("p (m t) -> p t m", t=PACK)
             th = work.tile([P, PACK, P], F32, bufs=LAG + 1)
             h = work.tile([P, PACK, P], F32, bufs=LAG + 3)
-            rt = work.tile([P, PACK, P], F32, bufs=LAG + 2)
             nc.scalar.activation(out=th[:], in_=pre, func=ACT.Tanh, scale=0.5)
             nc.scalar.activation(out=h[:], in_=pre, func=ACT.Silu)
-            if RT_ENGINE[s] != "v":
-                affine_on(RT_ENGINE[s], rt[:], th[:], tau_nh[:, i:i + 1], tau_h[:, i:i + 1])
+            if RT_ENGINE[s] == "s":
+                rt = work.tile([P, PACK, P], F32, bufs=LAG + 2)
+                affine_on("s", rt[:], th[:], tau_nh[:, i:i + 1], tau_h[:, i:i + 1])
+                live["rt", s] = rt
             live["th", s] = th
             live["h", s] = h
-            live["rt", s] = rt
 
-        def rt_on_vector(s):
+        def rt_on(engine, s):
             i = s // GROUPS
-            if RT_ENGINE[s] == "v":
-                affine_on("v", live["rt", s][:], live["th", s][:], tau_nh[:, i:i + 1], tau_h[:, i:i + 1])
+            if RT_ENGINE[s] == engine:
+                rt_late = work.tile([P, PACK, P], F32, bufs=RT_BUFS)
+                affine_on(engine, rt_late[:], live["th", s][:], tau_nh[:, i:i + 1], tau_h[:, i:i + 1])
+                live["rt", s] = rt_late
 
         def slope(s):
             x = work.tile([P, PACK, P], F32, bufs=2)
@@ -252,17 +268,26 @@ def tile_meanflowtangentresidual_kernel(tc, z, v, tau, gin, w1, gf, w2_bytes, w2
         def turn_hidden(s):
             y_bank = psum.tile([P, PACK, P], F32, bufs=2)
             for t in range(PACK):
-                nc.tensor.matmul(y_bank[:, t, :], lhsT=live["h", s][:, t, :], rhs=ident_f[:], start=True, stop=False,
+                nc.tensor.matmul(y_bank[:, t, :], lhsT=live["h", s][:, t, :], rhs=ident_f[:], start=(t == 0), stop=False,
                                  is_transpose=True)
-                nc.tensor.matmul(y_bank[:, t, :], lhsT=live["a", s][:, t, :], rhs=ident_f[:], start=False, stop=True,
-                                 is_transpose=True)
+            for t in range(PACK):
+                nc.tensor.matmul(y_bank[:, t, :], lhsT=live["a", s][:, t, :], rhs=ident_f[:], start=False,
+                                 stop=(t == PACK - 1), is_transpose=True)
             live["y_bank", s] = y_bank
 
         def gain_hidden(s):
             g = s % GROUPS
-            m_il = work.tile([P, P, PACK], BF16, bufs=2, align_bytes=64)
-            nc.vector.tensor_tensor(out=m_il[:], in0=live["y_bank", s][:].rearrange("p t n -> p n t"),
-                                    in1=gf_bf[:, g, :].unsqueeze(1).to_broadcast([P, P, PACK]), op=ALU.mult)
+            m_il = work.tile([P, P, PACK], BF16, bufs=3, align_bytes=64)
+            if GAIN_ENGINE[s] == "v":
+                nc.vector.tensor_tensor(out=m_il[:], in0=live["y_bank", s][:].rearrange("p t n -> p n t"),
+                                        in1=gf_bf[:, g, :].unsqueeze(1).to_broadcast([P, P, PACK]), op=ALU.mult)
+            else:
+                m_planes = work.tile([P, PACK, P], BF16, bufs=2)
+                for t in range(PACK):
+                    nc.scalar.activation(out=m_planes[:, t, :], in_=live["y_bank", s][:, t, :], func=ACT.Copy,
+                                         scale=gf_f[:, g, t:t + 1])
+                dst, src = interleaved(m_il[:], m_planes[:])
+                nc.scalar.copy(out=dst, in_=src)
             live["m_il", s] = m_il
 
         def m_quantize(s):
@@ -271,13 +296,13 @@ def tile_meanflowtangentresidual_kernel(tc, z, v, tau, gin, w1, gf, w2_bytes, w2
         def second_pass(s):
             i, g = divmod(s, GROUPS)
             if g == 0:
-                live["acc", i] = psum.tile([P, D], F32, bufs=2, name="acc", tag="acc")
+                live["acc", i] = psum.tile([P, D], F32, bufs=3 - D_BUFS, name="acc", tag="acc")
             nc.tensor.matmul_mx(out=live["acc", i][:], lhsT=m_codes[:, s, :].bitcast(FP8X4), lhsT_scale=m_scales[:, s, :],
                                 rhs=w2_codes[:, g, :].bitcast(FP8X4), rhs_scale=w2_scales[:, g, :],
                                 start=(g == 0), stop=(g == GROUPS - 1))
 
         def residual(i):
-            err = work.tile([P, D], F32, bufs=3)
+            err = work.tile([P, D], F32, bufs=4)
             nc.vector.tensor_tensor(out=err[:], in0=live["acc", i][:], in1=v_sb[i][:], op=ALU.subtract)
             live["err", i] = err
 
@@ -285,7 +310,7 @@ def tile_meanflowtangentresidual_kernel(tc, z, v, tau, gin, w1, gf, w2_bytes, w2
             squares = work.tile([P, D], BF16, bufs=2)
             total = work.tile([P, 1], F32, bufs=2)
             base = work.tile([P, 1], F32, bufs=2)
-            wgt = work.tile([P, 1], F32, bufs=2)
+            wgt = work.tile([P, 1], F32, bufs=3)
             nc.scalar.activation(out=squares[:], in_=live["err", i][:], func=ACT.Square, accum_out=total[:])
             nc.gpsimd.tensor_scalar(out=base[:], in0=total[:], scalar1=1.0 / D, scalar2=0.1, op0=ALU.mult, op1=ALU.add)
             nc.gpsimd.tensor_tensor(out=wgt[:], in0=base[:], in1=power[:], op=ALU.pow)
@@ -293,26 +318,32 @@ def tile_meanflowtangentresidual_kernel(tc, z, v, tau, gin, w1, gf, w2_bytes, w2
 
         def finish(i):
             result = work.tile([P, D], F32, bufs=2)
-            affine_on("v" if i == TILES - 1 else "g" if OUT_POOL else "s", result[:], live["err", i][:], live["wgt", i][:], None)
+            affine_on(OUT_ENGINE[i], result[:], live["err", i][:], live["wgt", i][:], None)
             nc.sync.dma_start(out=out_rows[:, i, :], in_=result[:])
 
         def at(k, first, period, count):
             n, rest = divmod(k - first, period)
             return [n] if rest == 0 and 0 <= n < count else []
 
+        for n in range(PRE_PIECES):
+            w2_piece(n)
         scale_v(0)
         turn_z(0)
-        turn_dz(0)
-        gain_in(0, 0)
+        turn_dz(0, 0)
+        turn_dz(0, 1)
         w1_interleave(0)
-        x_quantize_half(0, 0)
+        gain_in(0, 0)
         w1_quantize(0)
-        gain_in(0, 1)
+        x_quantize_half(0, 0)
         w1_interleave(1)
-        x_quantize_half(0, 1)
+        gain_in(0, 1)
         w1_quantize(1)
+        x_quantize_half(0, 1)
+        gf_f = keep.tile([P, GROUPS, PACK], F32)
+        if "s" in GAIN_ENGINE:
+            nc.vector.tensor_copy(out=gf_f[:], in_=gf_bf[:])
 
-        for n in range(HEAD_PIECES):
+        for n in range(PRE_PIECES, HEAD_PIECES):
             w2_piece(n)
         pieces = HEAD_PIECES
         w2_done = 0
@@ -323,7 +354,10 @@ def tile_meanflowtangentresidual_kernel(tc, z, v, tau, gin, w1, gf, w2_bytes, w2
         for k in range(-1, STEPS + FIN + 8):
             for s in at(k, 0, 1, STEPS):
                 activations(s)
-            for i in at(k, 0, GROUPS, TILES - 1):
+            for s in at(k, FIN, 1, STEPS):
+                if GAIN_ENGINE[s] == "s":
+                    gain_hidden(s)
+            for i in at(k, 0, GROUPS, V1_TILES - 1):
                 scale_v(i + 1)
             for g in range(2, GROUPS):
                 if W1_IL[g] != "v" and k == g - 3:
@@ -332,54 +366,62 @@ def tile_meanflowtangentresidual_kernel(tc, z, v, tau, gin, w1, gf, w2_bytes, w2
             while pieces < 2 * PACK * GROUPS and pieces < HEAD_PIECES + PIECE_RATE * (k + 1):
                 w2_piece(pieces)
                 pieces = pieces + 1
-            if k - 3 in closed and closed[k - 3] < TILES - 1:
-                finish(closed[k - 3])
             if k - 2 in closed:
                 weight(closed[k - 2])
+            if k - 3 in closed and OUT_ENGINE[closed[k - 3]] != "v":
+                finish(closed[k - 3])
             for s in at(k, LAG, 1, STEPS):
                 slope(s)
+            for s in at(k, LAG - 1, 1, STEPS):
+                rt_on("g", s)
             for s in at(k, FIN, 1, STEPS):
-                gain_hidden(s)
-            for g in at(k, 0, 1, 2):
-                w1_quantize(g + 2)
-            for s in at(k, LAG, 1, STEPS):
-                tangent(s)
-            for i in at(k, 1, GROUPS, TILES - 1):
-                gain_in(i + 1, 0)
-            for i in at(k, 2, GROUPS, TILES - 1):
-                gain_in(i + 1, 1)
-            for s in at(k, FIN, 1, STEPS):
-                m_quantize(s)
+                if GAIN_ENGINE[s] == "v":
+                    gain_hidden(s)
+            if k - 1 in closed:
+                residual(closed[k - 1])
             for g in range(2, GROUPS):
                 if W1_IL[g] == "v" and k == g - 3:
                     w1_interleave(g)
+            for i in at(k, 0, GROUPS, TILES - 1):
+                gain_in(i + 1, 0)
+            for i in at(k, 2, GROUPS, TILES - 1):
+                gain_in(i + 1, 1)
+            for s in at(k, LAG, 1, STEPS):
+                tangent(s)
+            for s in at(k, LAG - 1, 1, STEPS):
+                rt_on("v", s)
+            for s in at(k, FIN, 1, STEPS):
+                m_quantize(s)
             if before >= 2 * PACK * (w2_done + 1):
                 w2_quantize(w2_done)
                 w2_ready[w2_done] = k
                 w2_done = w2_done + 1
+            for g in range(2, GROUPS):
+                if k == g - (3 if W1_IL[g] == "v" else 2):
+                    w1_quantize(g)
             for i in at(k, 2, GROUPS, TILES - 1):
                 x_quantize(i + 1)
-            if k - 1 in closed:
-                residual(closed[k - 1])
-            if k - 3 in closed and closed[k - 3] == TILES - 1:
+            if k - 3 in closed and OUT_ENGINE[closed[k - 3]] == "v":
                 finish(closed[k - 3])
-            for s in at(k, LAG - 1, 1, STEPS):
-                rt_on_vector(s)
             for s in at(k, -1, 1, STEPS):
                 project(s, 0, "pre", 2)
-            for twice in range(2):
+            for s in at(k, LAG - 1, 1, STEPS if D_BUFS == 2 else 0):
+                project(s, 1, "dpre", 2)
+            for twice in range(PASSES):
                 s = next_pass
                 if s < STEPS and k > s + FIN and k > w2_ready.get(s % GROUPS, k) and k not in closed:
                     second_pass(s)
                     next_pass = s + 1
                     if s % GROUPS == GROUPS - 1:
                         closed[k] = s // GROUPS
-            for s in at(k, LAG - 1, 1, STEPS):
-                project(s, 1, "dpre", 1)
-            for i in at(k, 0, GROUPS, TILES - 1):
+            for i in at(k, -1, GROUPS, TILES - 1):
                 turn_z(i + 1)
+            for i in at(k, 0, GROUPS, TILES - 1):
+                turn_dz(i + 1, 0)
             for i in at(k, 1, GROUPS, TILES - 1):
-                turn_dz(i + 1)
+                turn_dz(i + 1, 1)
+            for s in at(k, LAG - 1, 1, STEPS if D_BUFS == 1 else 0):
+                project(s, 1, "dpre", 1)
             for s in at(k, LAG, 1, STEPS):
                 turn_hidden(s)
         assert next_pass == STEPS and len(closed) == TILES

@@ -27,16 +27,22 @@ OUT_ENGINE = "sssssssv"
 OUT_POOL = False
 W1_IL = "vvvv"
 W2_IL = "ssss"
-HEAD_PIECES = 12
+HEAD_PIECES = 8
 PIECE_RATE = 1
 LAG = 2
 YLAG = 2
-PASSES = 2
+PASSES = 3
 D_BUFS = 2
+Y_PRE = 0
+SPLIT_LAST = True
+HEAD_ORDER = 0
+EARLY_RATE = 3
+LATE_PIECES = 12
+A0_PARTS = 1
 RT_BUFS = 1
 GAIN_ENGINE = "v" * 32
-LOADS = "tau x0 a0 sc b0 gin a1 gf x1 a2 b1 a3 b2 b3 x2 x3 x4 x5 x6 x7"
-PRE_PIECES = 0
+LOADS = "tau sc b0 a0 x0 gin a1 gf b1 x1 a2 a3 b2 b3 x2 x3 x4 x5 x6 x7"
+PRE_PIECES = 3
 RT_ENGINE = "s" * 32
 
 
@@ -62,7 +68,9 @@ def tile_meanflowtangentresidual_kernel(tc, z, v, tau, gin, w1, gf, w2_bytes, w2
         w2_sc = keep.tile([P, GROUPS, PACK], F32)
         z_sb = [keep.tile([P, D], BF16, name="z%d" % i) for i in range(TILES)]
         v_sb = [keep.tile([P, D], BF16, name="v%d" % i) for i in range(TILES)]
-        w1_raw = [keep.tile([P, PACK, K_PASS], BF16, name="w1raw%d" % g) for g in range(GROUPS)]
+        parts = [A0_PARTS, 1, 1, 1]
+        w1_raw = [[keep.tile([P, PACK, K_PASS // parts[g]], BF16, name="w1raw%d_%d" % (g, c)) for c in range(parts[g])]
+                  for g in range(GROUPS)]
         w2_raw = [keep.tile([P, PACK * D], U8, name="w2raw%d" % g) for g in range(GROUPS)]
         w1_rows = w1.rearrange("(p j) f -> p j f", j=PACK)
         w2_rows = w2_bytes.rearrange("(g p t) n -> g p (t n)", p=P, t=PACK)
@@ -71,8 +79,11 @@ def tile_meanflowtangentresidual_kernel(tc, z, v, tau, gin, w1, gf, w2_bytes, w2
             nc.sync.dma_start(out=z_sb[i][:], in_=z_rows[:, i, :])
             nc.sync.dma_start(out=v_sb[i][:], in_=v_rows[:, i, :])
 
-        def load_w1(g):
-            nc.sync.dma_start(out=w1_raw[g][:], in_=w1_rows[:, :, g * K_PASS:(g + 1) * K_PASS])
+        def load_w1(g, only=None):
+            width = K_PASS // parts[g]
+            for c in (range(parts[g]) if only is None else [only]):
+                first = g * K_PASS + c * width
+                nc.sync.dma_start(out=w1_raw[g][c][:], in_=w1_rows[:, :, first:first + width])
 
         def load_w2(g):
             nc.sync.dma_start(out=w2_raw[g][:], in_=w2_rows[g])
@@ -86,6 +97,8 @@ def tile_meanflowtangentresidual_kernel(tc, z, v, tau, gin, w1, gf, w2_bytes, w2
                 nc.sync.dma_start(out=w2_sc[:], in_=w2_scale.rearrange("(g p t) o -> p g (t o)", p=P, t=PACK))
             elif item == "gf":
                 nc.sync.dma_start(out=gf_bf[:], in_=gf.rearrange("(g p t) -> p g t", p=P, t=PACK))
+            elif item.startswith("p"):
+                load_w1(0, int(item.replace("p", "")))
             elif item.startswith("a"):
                 load_w1(int(item.replace("a", "")))
             elif item.startswith("b"):
@@ -115,6 +128,9 @@ def tile_meanflowtangentresidual_kernel(tc, z, v, tau, gin, w1, gf, w2_bytes, w2
         nc.vector.tensor_tensor(out=diag[:], in0=ident_bf[:].unsqueeze(1).to_broadcast([P, TILES, P]),
                                 in1=tau_bf[:].unsqueeze(2).to_broadcast([P, TILES, P]), op=ALU.mult)
 
+        err = keep.tile([P, TILES, D + 8], F32)
+        nc.vector.tensor_scalar(out=err[:, :, D], in0=tau_bf[:], scalar1=0.0, scalar2=(0.1 * D) ** 0.5,
+                                op0=ALU.mult, op1=ALU.add)
         w1_codes = keep.tile([P, GROUPS, K_PASS], U32, align_bytes=64)
         w1_scales = keep.tile([P, GROUPS, K_PASS], U8, align_bytes=64)
         w2_codes = keep.tile([P, GROUPS, D], U32, align_bytes=64)
@@ -151,8 +167,10 @@ def tile_meanflowtangentresidual_kernel(tc, z, v, tau, gin, w1, gf, w2_bytes, w2
 
         def w1_interleave(g):
             w1_il = work.tile([P, K_PASS, PACK], BF16, bufs=2, align_bytes=64)
-            dst, src = interleaved(w1_il[:], w1_raw[g][:])
-            copy_on(W1_IL[g], dst, src)
+            width = K_PASS // parts[g]
+            for c in range(parts[g]):
+                dst, src = interleaved(w1_il[:, c * width:(c + 1) * width, :], w1_raw[g][c][:])
+                copy_on(W1_IL[g], dst, src)
             live["w1_il", g] = w1_il
 
         def w1_quantize(g):
@@ -266,7 +284,7 @@ def tile_meanflowtangentresidual_kernel(tc, z, v, tau, gin, w1, gf, w2_bytes, w2
             live["a", s] = a
 
         def turn_hidden(s):
-            y_bank = psum.tile([P, PACK, P], F32, bufs=2)
+            y_bank = psum.tile([P, PACK, P], F32, bufs=2, tag="pre" if s >= STEPS - Y_PRE else "y_bank")
             for t in range(PACK):
                 nc.tensor.matmul(y_bank[:, t, :], lhsT=live["h", s][:, t, :], rhs=ident_f[:], start=(t == 0), stop=False,
                                  is_transpose=True)
@@ -302,24 +320,32 @@ def tile_meanflowtangentresidual_kernel(tc, z, v, tau, gin, w1, gf, w2_bytes, w2
                                 start=(g == 0), stop=(g == GROUPS - 1))
 
         def residual(i):
-            err = work.tile([P, D], F32, bufs=4)
-            nc.vector.tensor_tensor(out=err[:], in0=live["acc", i][:], in1=v_sb[i][:], op=ALU.subtract)
-            live["err", i] = err
+            nc.vector.tensor_tensor(out=err[:, i, :D], in0=live["acc", i][:], in1=v_sb[i][:], op=ALU.subtract)
+
+        def squares_of(i):
+            squares = work.tile([P, D + 1], BF16, bufs=2)
+            total = work.tile([P, 1], F32, bufs=3)
+            nc.scalar.activation(out=squares[:], in_=err[:, i, :D + 1], func=ACT.Square, scale=D ** -0.5,
+                                 accum_out=total[:])
+            live["total", i] = total
 
         def weight(i):
-            squares = work.tile([P, D], BF16, bufs=2)
-            total = work.tile([P, 1], F32, bufs=2)
-            base = work.tile([P, 1], F32, bufs=2)
+            total = live["total", i]
             wgt = work.tile([P, 1], F32, bufs=3)
-            nc.scalar.activation(out=squares[:], in_=live["err", i][:], func=ACT.Square, accum_out=total[:])
-            nc.gpsimd.tensor_scalar(out=base[:], in0=total[:], scalar1=1.0 / D, scalar2=0.1, op0=ALU.mult, op1=ALU.add)
-            nc.gpsimd.tensor_tensor(out=wgt[:], in0=base[:], in1=power[:], op=ALU.pow)
+            nc.gpsimd.tensor_tensor(out=wgt[:], in0=total[:], in1=power[:], op=ALU.pow)
             live["wgt", i] = wgt
 
         def finish(i):
             result = work.tile([P, D], F32, bufs=2)
-            affine_on(OUT_ENGINE[i], result[:], live["err", i][:], live["wgt", i][:], None)
-            nc.sync.dma_start(out=out_rows[:, i, :], in_=result[:])
+            if SPLIT_LAST and i == TILES - 1:
+                other = work.tile([P, D // 2], F32, bufs=1)
+                affine_on("v", result[:, :D // 2], err[:, i, :D // 2], live["wgt", i][:], None)
+                nc.sync.dma_start(out=out_rows[:, i, :D // 2], in_=result[:, :D // 2])
+                affine_on("s", other[:], err[:, i, D // 2:D], live["wgt", i][:], None)
+                nc.scalar.dma_start(out=out_rows[:, i, D // 2:], in_=other[:])
+            else:
+                affine_on(OUT_ENGINE[i], result[:], err[:, i, :D], live["wgt", i][:], None)
+                nc.sync.dma_start(out=out_rows[:, i, :], in_=result[:])
 
         def at(k, first, period, count):
             n, rest = divmod(k - first, period)
@@ -332,13 +358,22 @@ def tile_meanflowtangentresidual_kernel(tc, z, v, tau, gin, w1, gf, w2_bytes, w2
         turn_dz(0, 0)
         turn_dz(0, 1)
         w1_interleave(0)
-        gain_in(0, 0)
-        w1_quantize(0)
-        x_quantize_half(0, 0)
-        w1_interleave(1)
-        gain_in(0, 1)
-        w1_quantize(1)
-        x_quantize_half(0, 1)
+        if HEAD_ORDER == 0:
+            gain_in(0, 0)
+            w1_quantize(0)
+            x_quantize_half(0, 0)
+            w1_interleave(1)
+            gain_in(0, 1)
+            w1_quantize(1)
+            x_quantize_half(0, 1)
+        else:
+            w1_quantize(0)
+            gain_in(0, 0)
+            w1_interleave(1)
+            x_quantize_half(0, 0)
+            gain_in(0, 1)
+            w1_quantize(1)
+            x_quantize_half(0, 1)
         gf_f = keep.tile([P, GROUPS, PACK], F32)
         if "s" in GAIN_ENGINE:
             nc.vector.tensor_copy(out=gf_f[:], in_=gf_bf[:])
@@ -351,7 +386,7 @@ def tile_meanflowtangentresidual_kernel(tc, z, v, tau, gin, w1, gf, w2_bytes, w2
         next_pass = 0
         closed = {}
         FIN = LAG + YLAG
-        for k in range(-1, STEPS + FIN + 8):
+        for k in range(-1, STEPS + FIN + 9):
             for s in at(k, 0, 1, STEPS):
                 activations(s)
             for s in at(k, FIN, 1, STEPS):
@@ -363,53 +398,59 @@ def tile_meanflowtangentresidual_kernel(tc, z, v, tau, gin, w1, gf, w2_bytes, w2
                 if W1_IL[g] != "v" and k == g - 3:
                     w1_interleave(g)
             before = pieces
-            while pieces < 2 * PACK * GROUPS and pieces < HEAD_PIECES + PIECE_RATE * (k + 1):
+            while pieces < 2 * PACK * GROUPS and pieces < min(HEAD_PIECES + EARLY_RATE * (k + 1), LATE_PIECES + PIECE_RATE * (k + 1)):
                 w2_piece(pieces)
                 pieces = pieces + 1
             if k - 2 in closed:
-                weight(closed[k - 2])
-            if k - 3 in closed and OUT_ENGINE[closed[k - 3]] != "v":
-                finish(closed[k - 3])
+                squares_of(closed[k - 2])
+            if k - 4 in closed and OUT_ENGINE[closed[k - 4]] != "v":
+                finish(closed[k - 4])
             for s in at(k, LAG, 1, STEPS):
                 slope(s)
-            for s in at(k, LAG - 1, 1, STEPS):
+            for s in at(k, LAG - RT_BUFS, 1, STEPS):
                 rt_on("g", s)
+            if k - 3 in closed:
+                weight(closed[k - 3])
             for s in at(k, FIN, 1, STEPS):
                 if GAIN_ENGINE[s] == "v":
                     gain_hidden(s)
             if k - 1 in closed:
                 residual(closed[k - 1])
-            for g in range(2, GROUPS):
-                if W1_IL[g] == "v" and k == g - 3:
-                    w1_interleave(g)
             for i in at(k, 0, GROUPS, TILES - 1):
                 gain_in(i + 1, 0)
+            for g in range(2, GROUPS):
+                if W1_IL[g] == "v" and k == g - 2:
+                    w1_interleave(g)
             for i in at(k, 2, GROUPS, TILES - 1):
                 gain_in(i + 1, 1)
             for s in at(k, LAG, 1, STEPS):
                 tangent(s)
             for s in at(k, LAG - 1, 1, STEPS):
                 rt_on("v", s)
+            for s in at(k, FIN + 1, 1, STEPS):
+                if GAIN_ENGINE[s] == "s":
+                    m_quantize(s)
             for s in at(k, FIN, 1, STEPS):
-                m_quantize(s)
+                if GAIN_ENGINE[s] == "v":
+                    m_quantize(s)
             if before >= 2 * PACK * (w2_done + 1):
                 w2_quantize(w2_done)
                 w2_ready[w2_done] = k
                 w2_done = w2_done + 1
             for g in range(2, GROUPS):
-                if k == g - (3 if W1_IL[g] == "v" else 2):
+                if k == g - 2:
                     w1_quantize(g)
             for i in at(k, 2, GROUPS, TILES - 1):
                 x_quantize(i + 1)
-            if k - 3 in closed and OUT_ENGINE[closed[k - 3]] == "v":
-                finish(closed[k - 3])
+            if k - 4 in closed and OUT_ENGINE[closed[k - 4]] == "v":
+                finish(closed[k - 4])
             for s in at(k, -1, 1, STEPS):
                 project(s, 0, "pre", 2)
             for s in at(k, LAG - 1, 1, STEPS if D_BUFS == 2 else 0):
                 project(s, 1, "dpre", 2)
             for twice in range(PASSES):
                 s = next_pass
-                if s < STEPS and k > s + FIN and k > w2_ready.get(s % GROUPS, k) and k not in closed:
+                if s < STEPS and k > s + FIN + (GAIN_ENGINE[s] == "s") and k > w2_ready.get(s % GROUPS, k) and k not in closed:
                     second_pass(s)
                     next_pass = s + 1
                     if s % GROUPS == GROUPS - 1:

@@ -40,7 +40,7 @@ EARLY_RATE = 3
 LATE_PIECES = 12
 A0_PARTS = 1
 RT_BUFS = 1
-GAIN_ENGINE = "v" * 32
+GAIN_ENGINE = "v"*28+"svsv"
 LOADS = "tau sc b0 a0 x0 gin a1 gf b1 x1 a2 a3 b2 b3 x2 x3 x4 x5 x6 x7"
 PRE_PIECES = 3
 RT_ENGINE = "s" * 32

from contextlib import ExitStack

import concourse.mybir as mybir
from concourse.masks import make_identity

N, D, F = 1024, 512, 2048
FLOPS = 3 * 2 * N * D * F

F32 = mybir.dt.float32
BF16 = mybir.dt.bfloat16
U32 = mybir.dt.uint32
U8 = mybir.dt.uint8
FP8 = mybir.dt.float8_e4m3fn
FP8X4 = mybir.dt.float8_e4m3fn_x4
ALU = mybir.AluOpType
ACT = mybir.ActivationFunctionType

P = 128
PACK = 4
K_PASS = P * PACK
TILES = N // P
GROUPS = F // K_PASS
STEPS = TILES * GROUPS
V1_POOL = False
V1_TILES = 1
OUT_ENGINE = "sssssssv"
OUT_POOL = False
W1_IL = "vvvv"
W2_IL = "ssss"
HEAD_PIECES = 8
PIECE_RATE = 1
LAG = 2
YLAG = 2
PASSES = 3
D_BUFS = 2
Y_PRE = 0
SPLIT_LAST = True
HEAD_ORDER = 0
EARLY_RATE = 3
LATE_PIECES = 12
A0_PARTS = 1
RT_BUFS = 1
GAIN_ENGINE = "v"*28+"svsv"
LOADS = "tau sc b0 a0 x0 gin a1 gf b1 x1 a2 a3 b2 b3 x2 x3 x4 x5 x6 x7"
PRE_PIECES = 3
RT_ENGINE = "s" * 32


def interleaved(dst, src):
    return (dst.rearrange("p (c i) t -> p c t i", i=4), src.rearrange("p t (c i) -> p c t i", i=4))


def tile_meanflowtangentresidual_kernel(tc, z, v, tau, gin, w1, gf, w2_bytes, w2_scale, out):
    nc = tc.nc
    z_rows = z.rearrange("(p i) d -> p i d", i=TILES)
    v_rows = v.rearrange("(p i) d -> p i d", i=TILES)
    out_rows = out.rearrange("(p i) d -> p i d", i=TILES)

    with ExitStack() as ctx:
        keep = ctx.enter_context(tc.tile_pool(name="keep", bufs=1))
        work = ctx.enter_context(tc.tile_pool(name="work", bufs=3))
        psum = ctx.enter_context(tc.psum_pool(name="psum", bufs=1))
        ctx.enter_context(tc.manual_schedule())

        tau_bf = keep.tile([P, TILES], BF16)
        gin_bf = keep.tile([P, PACK], BF16)
        gf_bf = keep.tile([P, GROUPS, PACK], BF16)
        w2_sc = keep.tile([P, GROUPS, PACK], F32)
        z_sb = [keep.tile([P, D], BF16, name="z%d" % i) for i in range(TILES)]
        v_sb = [keep.tile([P, D], BF16, name="v%d" % i) for i in range(TILES)]
        parts = [A0_PARTS, 1, 1, 1]
        w1_raw = [[keep.tile([P, PACK, K_PASS // parts[g]], BF16, name="w1raw%d_%d" % (g, c)) for c in range(parts[g])]
                  for g in range(GROUPS)]
        w2_raw = [keep.tile([P, PACK * D], U8, name="w2raw%d" % g) for g in range(GROUPS)]
        w1_rows = w1.rearrange("(p j) f -> p j f", j=PACK)
        w2_rows = w2_bytes.rearrange("(g p t) n -> g p (t n)", p=P, t=PACK)

        def load_tokens(i):
            nc.sync.dma_start(out=z_sb[i][:], in_=z_rows[:, i, :])
            nc.sync.dma_start(out=v_sb[i][:], in_=v_rows[:, i, :])

        def load_w1(g, only=None):
            width = K_PASS // parts[g]
            for c in (range(parts[g]) if only is None else [only]):
                first = g * K_PASS + c * width
                nc.sync.dma_start(out=w1_raw[g][c][:], in_=w1_rows[:, :, first:first + width])

        def load_w2(g):
            nc.sync.dma_start(out=w2_raw[g][:], in_=w2_rows[g])

        for item in LOADS.split():
            if item == "tau":
                nc.sync.dma_start(out=tau_bf[:], in_=tau.rearrange("(p i) -> p i", i=TILES))
            elif item == "gin":
                nc.sync.dma_start(out=gin_bf[:], in_=gin.rearrange("(p t) -> p t", t=PACK))
            elif item == "sc":
                nc.sync.dma_start(out=w2_sc[:], in_=w2_scale.rearrange("(g p t) o -> p g (t o)", p=P, t=PACK))
            elif item == "gf":
                nc.sync.dma_start(out=gf_bf[:], in_=gf.rearrange("(g p t) -> p g t", p=P, t=PACK))
            elif item.startswith("p"):
                load_w1(0, int(item.replace("p", "")))
            elif item.startswith("a"):
                load_w1(int(item.replace("a", "")))
            elif item.startswith("b"):
                load_w2(int(item.replace("b", "")))
            else:
                load_tokens(int(item.replace("x", "")))

        warm = keep.tile([P, 1], F32)
        warm_out = keep.tile([P, 1], F32)
        nc.vector.memset(warm[:], 0.0)
        nc.scalar.activation(out=warm_out[:], in_=warm[:], func=ACT.Silu)
        ident_bf = keep.tile([P, P], BF16)
        ident_f = keep.tile([P, P], F32)
        make_identity(nc, ident_bf[:])
        make_identity(nc, ident_f[:])
        power = keep.tile([P, 1], F32)
        nc.gpsimd.memset(power[:], -0.75)
        tau_f = keep.tile([P, TILES], F32)
        tau_1 = keep.tile([P, TILES], F32)
        tau_h = keep.tile([P, TILES], F32)
        tau_nh = keep.tile([P, TILES], F32)
        diag = keep.tile([P, TILES, P], BF16)
        nc.vector.tensor_scalar(out=tau_1[:], in0=tau_bf[:], scalar1=1.0, scalar2=None, op0=ALU.add)
        nc.vector.tensor_copy(out=tau_f[:], in_=tau_bf[:])
        nc.vector.tensor_scalar(out=tau_h[:], in0=tau_bf[:], scalar1=0.5, scalar2=None, op0=ALU.mult)
        nc.vector.tensor_scalar(out=tau_nh[:], in0=tau_bf[:], scalar1=-0.5, scalar2=None, op0=ALU.mult)
        nc.vector.tensor_tensor(out=diag[:], in0=ident_bf[:].unsqueeze(1).to_broadcast([P, TILES, P]),
                                in1=tau_bf[:].unsqueeze(2).to_broadcast([P, TILES, P]), op=ALU.mult)

        err = keep.tile([P, TILES, D + 8], F32)
        nc.vector.tensor_scalar(out=err[:, :, D], in0=tau_bf[:], scalar1=0.0, scalar2=(0.1 * D) ** 0.5,
                                op0=ALU.mult, op1=ALU.add)
        w1_codes = keep.tile([P, GROUPS, K_PASS], U32, align_bytes=64)
        w1_scales = keep.tile([P, GROUPS, K_PASS], U8, align_bytes=64)
        w2_codes = keep.tile([P, GROUPS, D], U32, align_bytes=64)
        w2_scales = keep.tile([P, GROUPS, D], U8, align_bytes=64)
        x_codes = keep.tile([P, TILES, 2 * P], U32, align_bytes=64)
        x_scales = keep.tile([P, TILES, 2 * P], U8, align_bytes=64)
        m_codes = keep.tile([P, STEPS, P], U32, align_bytes=64)
        m_scales = keep.tile([P, STEPS, P], U8, align_bytes=64)

        live = {}

        def quantize(codes, scales, values):
            nc.vector.quantize_mx(out=codes.bitcast(FP8X4), scales=scales, in_=values)

        def copy_on(engine, dst, src):
            if engine == "v":
                nc.vector.tensor_copy(out=dst, in_=src)
            elif engine == "s":
                nc.scalar.copy(out=dst, in_=src)
            else:
                nc.gpsimd.tensor_scalar(out=dst, in0=src, scalar1=1.0, scalar2=0.0, op0=ALU.mult, op1=ALU.add)

        def affine_on(engine, dst, src, scale, bias):
            if engine == "s" and bias is None:
                nc.scalar.activation(out=dst, in_=src, func=ACT.Copy, scale=scale)
            elif engine == "s":
                nc.scalar.activation(out=dst, in_=src, func=ACT.Identity, scale=scale, bias=bias)
            elif engine == "v":
                nc.vector.tensor_scalar(out=dst, in0=src, scalar1=scale, scalar2=0.0 if bias is None else bias,
                                        op0=ALU.mult, op1=ALU.add)
            else:
                nc.gpsimd.tensor_scalar(out=dst, in0=src, scalar1=scale, scalar2=0.0 if bias is None else bias,
                                        op0=ALU.mult, op1=ALU.add)

        def w1_interleave(g):
            w1_il = work.tile([P, K_PASS, PACK], BF16, bufs=2, align_bytes=64)
            width = K_PASS // parts[g]
            for c in range(parts[g]):
                dst, src = interleaved(w1_il[:, c * width:(c + 1) * width, :], w1_raw[g][c][:])
                copy_on(W1_IL[g], dst, src)
            live["w1_il", g] = w1_il

        def w1_quantize(g):
            quantize(w1_codes[:, g, :], w1_scales[:, g, :], live["w1_il", g][:].rearrange("p n t -> p (n t)"))

        def w2_piece(n):
            g, t = divmod(n, 2 * PACK)
            if t == 0:
                live["w2_wide", g] = work.tile([P, PACK, D], BF16, bufs=2, name="w2_wide")
            if t == PACK:
                live["w2_il", g] = work.tile([P, D, PACK], BF16, bufs=2, align_bytes=64, name="w2_il")
            if t < PACK:
                nc.scalar.activation(out=live["w2_wide", g][:, t, :], in_=w2_raw[g][:, t * D:(t + 1) * D].bitcast(FP8),
                                     func=ACT.Copy, scale=w2_sc[:, g, t:t + 1])
            else:
                cols = slice((t - PACK) * P, (t - PACK + 1) * P)
                dst, src = interleaved(live["w2_il", g][:, cols, :], live["w2_wide", g][:, :, cols])
                copy_on(W2_IL[g], dst, src)

        def w2_quantize(g):
            quantize(w2_codes[:, g, :], w2_scales[:, g, :], live["w2_il", g][:].rearrange("p n t -> p (n t)"))

        def scale_v(i):
            v1 = work.tile([P, PACK, P], F32, bufs=2)
            affine_on("g" if V1_POOL and i > 0 else "s", v1[:], v_sb[i][:].rearrange("p (m t) -> p t m", t=PACK),
                      tau_1[:, i:i + 1], None)
            live["v1", i] = v1

        def turn_z(i):
            x_bank = psum.tile([P, PACK, P], F32, tag="x_bank")
            for t in range(PACK):
                z_t = z_sb[i][:, t::PACK]
                nc.tensor.matmul(x_bank[:, t, :], lhsT=z_t, rhs=ident_bf[:], start=True, stop=False)
                nc.tensor.matmul(x_bank[:, t, :], lhsT=z_t, rhs=diag[:, i, :], start=False, stop=True)
            live["x_bank", i, 0] = x_bank

        def turn_dz(i, half):
            if half == 1:
                x_bank = live["x_bank", i, 1]
            elif i == 0:
                x_bank = psum.tile([P, PACK, P], F32, tag="acc", bufs=3 - D_BUFS)
            else:
                x_bank = psum.tile([P, PACK, P], F32, tag="x_bank")
            for t in range(2 * half, 2 * half + 2):
                nc.tensor.matmul(x_bank[:, t, :], lhsT=z_sb[i][:, t::PACK], rhs=ident_bf[:], start=True, stop=False)
                if i < V1_TILES:
                    nc.tensor.matmul(x_bank[:, t, :], lhsT=live["v1", i][:, t, :], rhs=ident_f[:], start=False, stop=True,
                                     is_transpose=True)
                else:
                    v_t = v_sb[i][:, t::PACK]
                    nc.tensor.matmul(x_bank[:, t, :], lhsT=v_t, rhs=ident_bf[:], start=False, stop=False)
                    nc.tensor.matmul(x_bank[:, t, :], lhsT=v_t, rhs=diag[:, i, :], start=False, stop=True)
            live["x_bank", i, 1] = x_bank

        def gain_in(i, which):
            if which == 0:
                live["x_il", i] = work.tile([P, 2, P, PACK], BF16, bufs=2, align_bytes=64, name="x_il")
            nc.vector.tensor_tensor(out=live["x_il", i][:, which, :, :],
                                    in0=live["x_bank", i, which][:].rearrange("p t n -> p n t"),
                                    in1=gin_bf[:].unsqueeze(1).to_broadcast([P, P, PACK]), op=ALU.mult)

        def x_quantize(i):
            quantize(x_codes[:, i, :], x_scales[:, i, :], live["x_il", i][:].rearrange("p o n t -> p (o n t)"))

        def x_quantize_half(i, which):
            cols = slice(which * P, (which + 1) * P)
            quantize(x_codes[:, i, cols], x_scales[:, i, cols], live["x_il", i][:, which].rearrange("p n t -> p (n t)"))

        def project(s, which, tag, bufs):
            i, g = divmod(s, GROUPS)
            bank = psum.tile([P, K_PASS], F32, tag=tag, bufs=bufs, name=tag)
            cols = slice(which * P, (which + 1) * P)
            nc.tensor.matmul_mx(out=bank[:], lhsT=x_codes[:, i, cols].bitcast(FP8X4), lhsT_scale=x_scales[:, i, cols],
                                rhs=w1_codes[:, g, :].bitcast(FP8X4), rhs_scale=w1_scales[:, g, :],
                                start=True, stop=True)
            live[tag, s] = bank

        def activations(s):
            i = s // GROUPS
            pre = live["pre", s][:].rearrange("p (m t) -> p t m", t=PACK)
            th = work.tile([P, PACK, P], F32, bufs=LAG + 1)
            h = work.tile([P, PACK, P], F32, bufs=LAG + 3)
            nc.scalar.activation(out=th[:], in_=pre, func=ACT.Tanh, scale=0.5)
            nc.scalar.activation(out=h[:], in_=pre, func=ACT.Silu)
            if RT_ENGINE[s] == "s":
                rt = work.tile([P, PACK, P], F32, bufs=LAG + 2)
                affine_on("s", rt[:], th[:], tau_nh[:, i:i + 1], tau_h[:, i:i + 1])
                live["rt", s] = rt
            live["th", s] = th
            live["h", s] = h

        def rt_on(engine, s):
            i = s // GROUPS
            if RT_ENGINE[s] == engine:
                rt_late = work.tile([P, PACK, P], F32, bufs=RT_BUFS)
                affine_on(engine, rt_late[:], live["th", s][:], tau_nh[:, i:i + 1], tau_h[:, i:i + 1])
                live["rt", s] = rt_late

        def slope(s):
            x = work.tile([P, PACK, P], F32, bufs=2)
            nc.vector.scalar_tensor_tensor(out=x[:], in0=live["h", s][:], scalar=-1.0, in1=live["rt", s][:],
                                           op0=ALU.add, op1=ALU.mult)
            live["x", s] = x

        def tangent(s):
            i = s // GROUPS
            a = work.tile([P, PACK, P], F32, bufs=3)
            nc.vector.scalar_tensor_tensor(out=a[:], in0=live["x", s][:], scalar=tau_f[:, i:i + 1],
                                           in1=live["dpre", s][:].rearrange("p (m t) -> p t m", t=PACK),
                                           op0=ALU.add, op1=ALU.mult)
            live["a", s] = a

        def turn_hidden(s):
            y_bank = psum.tile([P, PACK, P], F32, bufs=2, tag="pre" if s >= STEPS - Y_PRE else "y_bank")
            for t in range(PACK):
                nc.tensor.matmul(y_bank[:, t, :], lhsT=live["h", s][:, t, :], rhs=ident_f[:], start=(t == 0), stop=False,
                                 is_transpose=True)
            for t in range(PACK):
                nc.tensor.matmul(y_bank[:, t, :], lhsT=live["a", s][:, t, :], rhs=ident_f[:], start=False,
                                 stop=(t == PACK - 1), is_transpose=True)
            live["y_bank", s] = y_bank

        def gain_hidden(s):
            g = s % GROUPS
            m_il = work.tile([P, P, PACK], BF16, bufs=3, align_bytes=64)
            if GAIN_ENGINE[s] == "v":
                nc.vector.tensor_tensor(out=m_il[:], in0=live["y_bank", s][:].rearrange("p t n -> p n t"),
                                        in1=gf_bf[:, g, :].unsqueeze(1).to_broadcast([P, P, PACK]), op=ALU.mult)
            else:
                m_planes = work.tile([P, PACK, P], BF16, bufs=2)
                for t in range(PACK):
                    nc.scalar.activation(out=m_planes[:, t, :], in_=live["y_bank", s][:, t, :], func=ACT.Copy,
                                         scale=gf_f[:, g, t:t + 1])
                dst, src = interleaved(m_il[:], m_planes[:])
                nc.scalar.copy(out=dst, in_=src)
            live["m_il", s] = m_il

        def m_quantize(s):
            quantize(m_codes[:, s, :], m_scales[:, s, :], live["m_il", s][:].rearrange("p n t -> p (n t)"))

        def second_pass(s):
            i, g = divmod(s, GROUPS)
            if g == 0:
                live["acc", i] = psum.tile([P, D], F32, bufs=3 - D_BUFS, name="acc", tag="acc")
            nc.tensor.matmul_mx(out=live["acc", i][:], lhsT=m_codes[:, s, :].bitcast(FP8X4), lhsT_scale=m_scales[:, s, :],
                                rhs=w2_codes[:, g, :].bitcast(FP8X4), rhs_scale=w2_scales[:, g, :],
                                start=(g == 0), stop=(g == GROUPS - 1))

        def residual(i):
            nc.vector.tensor_tensor(out=err[:, i, :D], in0=live["acc", i][:], in1=v_sb[i][:], op=ALU.subtract)

        def squares_of(i):
            squares = work.tile([P, D + 1], BF16, bufs=2)
            total = work.tile([P, 1], F32, bufs=3)
            nc.scalar.activation(out=squares[:], in_=err[:, i, :D + 1], func=ACT.Square, scale=D ** -0.5,
                                 accum_out=total[:])
            live["total", i] = total

        def weight(i):
            total = live["total", i]
            wgt = work.tile([P, 1], F32, bufs=3)
            nc.gpsimd.tensor_tensor(out=wgt[:], in0=total[:], in1=power[:], op=ALU.pow)
            live["wgt", i] = wgt

        def finish(i):
            result = work.tile([P, D], F32, bufs=2)
            if SPLIT_LAST and i == TILES - 1:
                other = work.tile([P, D // 2], F32, bufs=1)
                affine_on("v", result[:, :D // 2], err[:, i, :D // 2], live["wgt", i][:], None)
                nc.sync.dma_start(out=out_rows[:, i, :D // 2], in_=result[:, :D // 2])
                affine_on("s", other[:], err[:, i, D // 2:D], live["wgt", i][:], None)
                nc.scalar.dma_start(out=out_rows[:, i, D // 2:], in_=other[:])
            else:
                affine_on(OUT_ENGINE[i], result[:], err[:, i, :D], live["wgt", i][:], None)
                nc.sync.dma_start(out=out_rows[:, i, :], in_=result[:])

        def at(k, first, period, count):
            n, rest = divmod(k - first, period)
            return [n] if rest == 0 and 0 <= n < count else []

        for n in range(PRE_PIECES):
            w2_piece(n)
        scale_v(0)
        turn_z(0)
        turn_dz(0, 0)
        turn_dz(0, 1)
        w1_interleave(0)
        if HEAD_ORDER == 0:
            gain_in(0, 0)
            w1_quantize(0)
            x_quantize_half(0, 0)
            w1_interleave(1)
            gain_in(0, 1)
            w1_quantize(1)
            x_quantize_half(0, 1)
        else:
            w1_quantize(0)
            gain_in(0, 0)
            w1_interleave(1)
            x_quantize_half(0, 0)
            gain_in(0, 1)
            w1_quantize(1)
            x_quantize_half(0, 1)
        gf_f = keep.tile([P, GROUPS, PACK], F32)
        if "s" in GAIN_ENGINE:
            nc.vector.tensor_copy(out=gf_f[:], in_=gf_bf[:])

        for n in range(PRE_PIECES, HEAD_PIECES):
            w2_piece(n)
        pieces = HEAD_PIECES
        w2_done = 0
        w2_ready = {}
        next_pass = 0
        closed = {}
        FIN = LAG + YLAG
        for k in range(-1, STEPS + FIN + 9):
            for s in at(k, 0, 1, STEPS):
                activations(s)
            for s in at(k, FIN, 1, STEPS):
                if GAIN_ENGINE[s] == "s":
                    gain_hidden(s)
            for i in at(k, 0, GROUPS, V1_TILES - 1):
                scale_v(i + 1)
            for g in range(2, GROUPS):
                if W1_IL[g] != "v" and k == g - 3:
                    w1_interleave(g)
            before = pieces
            while pieces < 2 * PACK * GROUPS and pieces < min(HEAD_PIECES + EARLY_RATE * (k + 1), LATE_PIECES + PIECE_RATE * (k + 1)):
                w2_piece(pieces)
                pieces = pieces + 1
            if k - 2 in closed:
                squares_of(closed[k - 2])
            if k - 4 in closed and OUT_ENGINE[closed[k - 4]] != "v":
                finish(closed[k - 4])
            for s in at(k, LAG, 1, STEPS):
                slope(s)
            for s in at(k, LAG - RT_BUFS, 1, STEPS):
                rt_on("g", s)
            if k - 3 in closed:
                weight(closed[k - 3])
            for s in at(k, FIN, 1, STEPS):
                if GAIN_ENGINE[s] == "v":
                    gain_hidden(s)
            if k - 1 in closed:
                residual(closed[k - 1])
            for i in at(k, 0, GROUPS, TILES - 1):
                gain_in(i + 1, 0)
            for g in range(2, GROUPS):
                if W1_IL[g] == "v" and k == g - 2:
                    w1_interleave(g)
            for i in at(k, 2, GROUPS, TILES - 1):
                gain_in(i + 1, 1)
            for s in at(k, LAG, 1, STEPS):
                tangent(s)
            for s in at(k, LAG - 1, 1, STEPS):
                rt_on("v", s)
            for s in at(k, FIN + 1, 1, STEPS):
                if GAIN_ENGINE[s] == "s":
                    m_quantize(s)
            for s in at(k, FIN, 1, STEPS):
                if GAIN_ENGINE[s] == "v":
                    m_quantize(s)
            if before >= 2 * PACK * (w2_done + 1):
                w2_quantize(w2_done)
                w2_ready[w2_done] = k
                w2_done = w2_done + 1
            for g in range(2, GROUPS):
                if k == g - 2:
                    w1_quantize(g)
            for i in at(k, 2, GROUPS, TILES - 1):
                x_quantize(i + 1)
            if k - 4 in closed and OUT_ENGINE[closed[k - 4]] == "v":
                finish(closed[k - 4])
            for s in at(k, -1, 1, STEPS):
                project(s, 0, "pre", 2)
            for s in at(k, LAG - 1, 1, STEPS if D_BUFS == 2 else 0):
                project(s, 1, "dpre", 2)
            for twice in range(PASSES):
                s = next_pass
                if s < STEPS and k > s + FIN + (GAIN_ENGINE[s] == "s") and k > w2_ready.get(s % GROUPS, k) and k not in closed:
                    second_pass(s)
                    next_pass = s + 1
                    if s % GROUPS == GROUPS - 1:
                        closed[k] = s // GROUPS
            for i in at(k, -1, GROUPS, TILES - 1):
                turn_z(i + 1)
            for i in at(k, 0, GROUPS, TILES - 1):
                turn_dz(i + 1, 0)
            for i in at(k, 1, GROUPS, TILES - 1):
                turn_dz(i + 1, 1)
            for s in at(k, LAG - 1, 1, STEPS if D_BUFS == 1 else 0):
                project(s, 1, "dpre", 1)
            for s in at(k, LAG, 1, STEPS):
                turn_hidden(s)
        assert next_pass == STEPS and len(closed) == TILES
